import numpy as np
import ml_dtypes


def mxq(x, axis, fmt="e4m3"):
    dtype, down = {"e4m3": (ml_dtypes.float8_e4m3fn, 7), "e5m2": (ml_dtypes.float8_e5m2, 14)}[fmt]
    v = np.moveaxis(np.asarray(x, np.float32).astype(ml_dtypes.bfloat16).astype(np.float64), axis, -1)
    blocks = v.reshape(v.shape[:-1] + (-1, 32))
    amax = np.abs(blocks).max(-1, keepdims=True)
    byte = np.maximum(np.where(amax > 0, np.frexp(amax)[1] - 1 + 127, 0) - down, 1)
    scale = np.exp2(byte - 127.0)
    codes = (blocks / scale).astype(np.float32).astype(dtype).astype(np.float64)
    return np.moveaxis((codes * scale).reshape(v.shape), -1, axis)


WIDE = False


def mx_kscale(k):
    if not WIDE:
        return np.ones(k)
    levels = np.array([30, -30])
    if k % 512:
        return np.exp2(np.random.permutation(np.resize(levels, k // 32))).repeat(32)
    a = np.empty((k // 512, 16))
    for p in range(k // 512):
        a[p, :8] = np.random.permutation(np.resize(levels, 8))
        for g in range(8):
            far = levels[np.abs(levels - a[p, g]) >= 10]
            a[p, g + 8] = far[np.random.randint(len(far))]
    return np.exp2(a.ravel()).repeat(32)


def f64(x):
    return np.asarray(x).astype(np.float64)


def striped(idx):
    return np.tile(np.asarray(idx).reshape(-1, 16).T, (8, 1)).astype(np.uint16)


def unstriped(offs):
    return offs[:16].T.reshape(-1).astype(np.int64)


E2M1 = np.array([0.0, 0.5, 1.0, 1.5, 2.0, 3.0, 4.0, 6.0, -0.0, -0.5, -1.0, -1.5, -2.0, -3.0, -4.0, -6.0])


def pack_weight(w, fmt):
    k, n = w.shape
    w = f64(np.asarray(w, np.float32).astype(ml_dtypes.bfloat16)).reshape(k // 32, 32, n)
    amax = np.abs(w).max(1)
    if fmt in ("e4m3", "e5m2"):
        byte = np.frexp(amax)[1] - 1 + 127 - (7 if fmt == "e4m3" else 14)
    else:
        mant, ex = np.frexp(amax / 6.0)
        byte = np.where(mant > 0.5, ex, ex - 1) + 127
    byte = np.clip(np.where(amax > 0, byte, 1), 1, 254)
    scaled = (w * np.exp2(127.0 - byte)[:, None, :]).reshape(k, n).astype(np.float32)
    by_word = np.ascontiguousarray(scaled.reshape(k // 512, 128, 4, n).transpose(0, 1, 3, 2))
    if fmt in ("e4m3", "e5m2"):
        words = by_word.astype(ml_dtypes.float8_e4m3fn if fmt == "e4m3" else ml_dtypes.float8_e5m2).view(np.uint8)
    else:
        c = by_word.astype(ml_dtypes.float4_e2m1fn).view(np.uint8) & 0xF
        words = (c[..., 0::2] | (c[..., 1::2] << 4)).reshape(k // 512, 128, 2 * n)
    return np.ascontiguousarray(words), np.ascontiguousarray(byte.astype(np.uint8).reshape(k // 512, 16, n))


def unpack_weight(words, scales, fmt):
    g, _, n = scales.shape
    words = np.ascontiguousarray(words).reshape(g, 128, n, -1)
    if fmt in ("e4m3", "e5m2"):
        vals = words.view(ml_dtypes.float8_e4m3fn if fmt == "e4m3" else ml_dtypes.float8_e5m2).astype(np.float64)
    else:
        nib = np.empty((g, 128, n, 4), np.uint8)
        nib[..., 0::2] = words & 0xF
        nib[..., 1::2] = words >> 4
        vals = E2M1[nib]
    vals = vals * np.repeat(np.exp2(scales.astype(np.float64) - 127.0), 8, axis=1)[..., None]
    return vals.transpose(0, 1, 3, 2).reshape(g * 512, n)


def sigmoid(v):
    return 1.0 / (1.0 + np.exp(-v))


def e4m3fn_bytes(y):
    return np.clip(np.asarray(y, np.float64), -448.0, 448.0).astype(np.float32).astype(ml_dtypes.float8_e4m3fn).view(np.uint8)


def e4m3fn_values(b):
    return np.asarray(b, np.uint8).view(ml_dtypes.float8_e4m3fn).astype(np.float64)


def sgn(shape):
    return np.random.uniform(0.5, 2.0, shape) * np.where(np.random.standard_normal(shape) < 0, -1.0, 1.0)


K, T, J, R, V, N, E = 512, 1024, 256, 512, 1024, 256, 512


def setup_inputs():
    n = np.random.standard_normal
    idx = np.random.permutation(T)[:J]
    idx2 = np.random.permutation(V)[:J]
    idx3 = np.random.permutation(E)[:J]
    fk = mx_kscale(K)
    fr = mx_kscale(R)
    xtp = pack_weight(n((K, T)) / fk[:, None], "e2m1")
    wp = pack_weight(n((K, R)) * 1 / np.sqrt(K) * fk[:, None] * fr, "e5m2")
    w2p = pack_weight(n((K, R)) * 1 / np.sqrt(K) * fk[:, None] * fr, "e4m3")
    wbp = pack_weight(n((R, N)) * 1 / np.sqrt(R) / fr[:, None], "e4m3")
    return {
        "xt_words": xtp[0],
        "xt_scales": xtp[1],
        "w_words": wp[0],
        "w_scales": wp[1],
        "w2_words": w2p[0],
        "w2_scales": w2p[1],
        "ca": e4m3fn_bytes(60.0 * n((R, V))),
        "st": (np.random.uniform(0.015, 0.045, (R, 1))).astype(np.float32),
        "wb_words": wbp[0],
        "wb_scales": wbp[1],
        "so": (sgn((N, 1))).astype(np.float32),
        "offs": striped(idx),
        "offs2": striped(idx2),
        "offs3": striped(idx3),
    }


def reference(xt_words, xt_scales, w_words, w_scales, w2_words, w2_scales, ca, st, wb_words, wb_scales, so, offs, offs2, offs3):
    idx = unstriped(offs)
    idx2 = unstriped(offs2)
    idx3 = unstriped(offs3)
    xtu = unpack_weight(xt_words, xt_scales, "e2m1")
    wu = unpack_weight(w_words, w_scales, "e5m2")
    w2u = unpack_weight(w2_words, w2_scales, "e4m3")
    wbu = unpack_weight(wb_words, wb_scales, "e4m3")
    xtidxg = xtu[:, idx]
    a = wu.T @ xtidxg
    b = w2u.T @ xtidxg
    g1 = sigmoid(e4m3fn_values(ca)[:, idx2] * f64(st))
    hid = b + g1 * (a - b)
    hidq = mxq(hid, 0, "e5m2")
    p = wbu.T @ hidq
    y = np.zeros((N, E))
    y[:, idx3] = p * f64(so)
    return y

@@ -1,0 +1,202 @@
+from contextlib import ExitStack
+
+import concourse.mybir as mybir
+
+K, T, J, R, V, N, E = 512, 1024, 256, 512, 1024, 256, 512
+FLOPS = 2 * K * R * J * 2 + 2 * R * N * J
+
+F32 = mybir.dt.float32
+BF16 = mybir.dt.bfloat16
+I32 = mybir.dt.int32
+U32 = mybir.dt.uint32
+U16 = mybir.dt.uint16
+U8 = mybir.dt.uint8
+FP8 = mybir.dt.float8_e4m3fn
+E4M3X4 = mybir.dt.float8_e4m3fn_x4
+E5M2X4 = mybir.dt.float8_e5m2_x4
+E2M1X4 = mybir.dt.float4_e2m1fn_x4
+ACT = mybir.ActivationFunctionType
+ALU = mybir.AluOpType
+
+P = 128
+PACK = 4
+HALF = 128
+CHUNK = 64
+LIST_ROWS = 16
+
+
+def tile_list_softchoice_kernel(tc, xt_words, xt_scales, w_words, w_scales, w2_words, w2_scales,
+                                    ca, st, wb_words, wb_scales, so, offs, offs2, offs3, out):
+    nc = tc.nc
+    halves = J // HALF
+    chunks = J // CHUNK
+    with ExitStack() as ctx:
+        held = ctx.enter_context(tc.tile_pool(name="held", bufs=1))
+        psum = ctx.enter_context(tc.psum_pool(name="psum", bufs=1))
+
+        tok_list = held.tile([P, J // LIST_ROWS], U16, name="tok_list")
+        entry_list = held.tile([P, J // LIST_ROWS], U16, name="entry_list")
+        col_list = held.tile([P, J // LIST_ROWS], U16, name="col_list")
+        x_words = held.tile([P, T], U16, name="x_words", align_bytes=64)
+        x_plane = held.tile([P, T], U8, name="x_plane", align_bytes=64)
+        store = [held.tile([P, V], U8, name=f"store{t}", align_bytes=64) for t in range(PACK)]
+        w_raw = [held.tile([P, R], I32, name=f"w_raw{m}", align_bytes=64) for m in range(2)]
+        w_rows = [held.tile([P, 2 * R], U8, name=f"w_rows{m}", align_bytes=64) for m in range(2)]
+        x_rows = held.tile([4, 4 * T], U8, name="x_rows", align_bytes=64)
+        wb_sb = held.tile([P, N], I32, name="wb_sb", align_bytes=64)
+        wb_rows = held.tile([P, N], U8, name="wb_rows", align_bytes=64)
+        steps = held.tile([P, PACK], F32, name="steps")
+        gains = held.tile([P, N // P], F32, name="gains")
+        pages = [held.tile([P, E], F32, name=f"page{n}") for n in range(N // P)]
+        hid_words = held.tile([P, CHUNK + J], I32, name="hid_words", align_bytes=64)
+        hid_plane = held.tile([P, CHUNK + J], U8, name="hid_plane", align_bytes=64)
+
+        nc.vector.memset(x_plane[:].bitcast(I32), 0)
+        for rows in (w_rows[0], w_rows[1], wb_rows):
+            nc.vector.memset(rows[:].bitcast(I32), 0)
+        nc.vector.memset(hid_words[:, 0:CHUNK], 0)
+        nc.vector.memset(hid_plane[:, 0:CHUNK].bitcast(I32), 0)
+        for page in pages:
+            nc.vector.memset(page[:], 0.0)
+
+        def load_words(tile, words):
+            nc.sync.dma_start(tile[:], words[0].rearrange("p n t -> p (n t)").bitcast(I32))
+
+        def load_rows(engine, rows, scales):
+            src = scales[0].bitcast(I32).rearrange("(a b r) c -> b r a c", a=2, b=2)
+            for b in range(2):
+                engine.dma_start(rows[32 * b : 32 * b + 4, :].bitcast(I32).rearrange("p (a c) -> p a c", a=2), src[b])
+
+        def spread_rows(rows, width):
+            words = rows[:].bitcast(I32)
+            nc.vector.tensor_copy(words[64:128, 0 : width // 4], words[0:64, width // 4 : width // 2])
+
+        ca_dealt = ca.rearrange("(p t) v -> t p v", t=PACK)
+        nc.sync.dma_start(x_rows[:].bitcast(I32).rearrange("r (q c) -> r q c", q=4), xt_scales[0].bitcast(I32).rearrange("(q r) c -> r q c", q=4))
+        nc.sync.dma_start(tok_list[:], offs)
+        nc.sync.dma_start(x_words[:].bitcast(I32), xt_words[0].bitcast(I32))
+        nc.sync.dma_start(entry_list[:], offs2)
+        nc.sync.dma_start(store[0][:], ca_dealt[0])
+        load_words(w_raw[0], w_words)
+        load_words(w_raw[1], w2_words)
+        nc.sync.dma_start(store[1][:], ca_dealt[1])
+        nc.gpsimd.dma_start(steps[:], st.rearrange("(p t) o -> p (t o)", t=PACK))
+        load_rows(nc.sync, w_rows[0], w_scales)
+        load_rows(nc.sync, w_rows[1], w2_scales)
+        nc.sync.dma_start(store[2][:], ca_dealt[2])
+        nc.sync.dma_start(store[3][:], ca_dealt[3])
+        load_words(wb_sb, wb_words)
+        nc.sync.dma_start(col_list[:], offs3)
+        for q in range(4):
+            nc.sync.dma_start(wb_rows[32 * q : 32 * q + 4, :].bitcast(I32), wb_scales[0, 4 * q : 4 * q + 4, :].bitcast(I32))
+        with nc.allow_non_contiguous_dma(reason="one value a partition"):
+            nc.sync.dma_start(gains[:], so.rearrange("(h p) o -> p (h o)", p=P))
+
+        xg_words = held.tile([P, J], U16, name="xg_words", align_bytes=64)
+        xg_plane = held.tile([P, J], U8, name="xg_plane", align_bytes=64)
+        for q in range(4):
+            nc.vector.tensor_copy(x_plane[32 * q : 32 * q + 4, :].bitcast(I32), x_rows[:, q * T : (q + 1) * T].bitcast(I32))
+        nc.vector.tensor_copy(xg_words[:], x_words[:].indirect(tok_list[:]))
+        nc.vector.tensor_copy(xg_plane[:], x_plane[:].indirect(tok_list[:]))
+
+        w_dealt = [held.tile([P, R], U32, name=f"w_dealt{m}", align_bytes=64) for m in range(2)]
+        w_plane = [held.tile([P, R], U8, name=f"w_plane{m}", align_bytes=64) for m in range(2)]
+        sums = [[psum.tile([P, PACK, HALF], F32, name=f"sums{m}_{h}") for h in range(halves)] for m in range(2)]
+        share = [held.tile([P, CHUNK, PACK], F32, name=f"share{c}") for c in range(chunks)]
+
+        def first_products(m, h):
+            cols = slice(h * HALF, (h + 1) * HALF)
+            for t in range(PACK):
+                nc.tensor.matmul_mx(sums[m][h][:, t, :], lhsT=w_dealt[m][:, t * P : (t + 1) * P].bitcast((E5M2X4, E4M3X4)[m]),
+                                    lhsT_scale=w_plane[m][:, t * P : (t + 1) * P],
+                                    rhs=xg_words[:, cols].bitcast(E2M1X4), rhs_scale=xg_plane[:, cols],
+                                    start=True, stop=True)
+
+        picked = [held.tile([P, PACK * HALF], U8, name=f"picked{h}") for h in range(halves)]
+        logits = [held.tile([P, PACK, HALF], F32, name=f"logits{h}") for h in range(halves)]
+
+        def look_up(t, h):
+            entries = entry_list[:, h * HALF // LIST_ROWS : (h + 1) * HALF // LIST_ROWS]
+            part = slice(t * HALF, (t + 1) * HALF)
+            nc.vector.tensor_copy(picked[h][:, part], store[t][:].indirect(entries))
+            nc.scalar.activation(logits[h][:, t, :], picked[h][:, part].bitcast(FP8), ACT.Copy, scale=steps[:, t : t + 1])
+
+        def shares(h):
+            for u in range(HALF // CHUNK):
+                nc.scalar.activation(share[h * HALF // CHUNK + u][:].rearrange("p (c i) t -> p c t i", i=4),
+                                     logits[h][:, :, u * CHUNK : (u + 1) * CHUNK].rearrange("p t (c i) -> p c t i", i=4),
+                                     ACT.Sigmoid)
+
+        def deal_words(m):
+            nc.scalar.copy(w_dealt[m][:].rearrange("p (t q) -> p q t", t=PACK),
+                           w_raw[m][:].bitcast(U32).rearrange("p (q t) -> p q t", t=PACK))
+
+        def deal_scales(m):
+            spread_rows(w_rows[m], R)
+            nc.vector.tensor_copy(w_plane[m][:].rearrange("p (t q) -> p q t", t=PACK),
+                                  w_rows[m][:, 0:R].rearrange("p (q t) -> p q t", t=PACK))
+
+        deal_words(0)
+        deal_words(1)
+        for t in (0, 1):
+            for h in range(halves):
+                look_up(t, h)
+        deal_scales(0)
+        deal_scales(1)
+        for h in range(halves):
+            for m in range(2):
+                first_products(m, h)
+        for h in range(halves):
+            for t in (2, 3):
+                look_up(t, h)
+            shares(h)
+
+        kept = [held.tile([P, CHUNK, PACK], F32, name=f"kept{c}") for c in range(4)] * chunks
+        rest = [held.tile([P, CHUNK, PACK], F32, name=f"rest{c}") for c in range(4)] * chunks
+        hid = [held.tile([P, CHUNK * PACK], BF16, name=f"hid{c}", align_bytes=64) for c in range(chunks)]
+
+        def chunk_sums(m, c):
+            h, u = divmod(c, HALF // CHUNK)
+            return sums[m][h][:, :, u * CHUNK : (u + 1) * CHUNK].rearrange("p t j -> p j t")
+
+        def weigh_first(c):
+            nc.vector.tensor_tensor(kept[c][:], chunk_sums(0, c), share[c][:], ALU.mult)
+
+        def weigh_second(c):
+            nc.vector.scalar_tensor_tensor(rest[c][:], share[c][:], 1.0, chunk_sums(1, c), ALU.subtract, ALU.mult)
+
+        def join(c):
+            engine = nc.vector
+            engine.tensor_tensor(hid[c][:], kept[c][:].rearrange("p j t -> p (j t)"), rest[c][:].rearrange("p j t -> p (j t)"), ALU.subtract)
+
+        def finish(c):
+            own = slice((c + 1) * CHUNK, (c + 2) * CHUNK)
+            window = slice(c * CHUNK, (c + 2) * CHUNK)
+            nc.vector.quantize_mx(hid_words[:, own].bitcast(E5M2X4), hid_plane[:, own], hid[c][:])
+            prod = psum.tile([P, N // P, 2 * CHUNK], F32, name=f"prod{c}")
+            for n in range(N // P):
+                nc.tensor.matmul_mx(prod[:, n, :], lhsT=wb_sb[:, n * P : (n + 1) * P].bitcast(E4M3X4),
+                                    lhsT_scale=wb_rows[:, n * P : (n + 1) * P],
+                                    rhs=hid_words[:, window].bitcast(E5M2X4), rhs_scale=hid_plane[:, window],
+                                    start=True, stop=True)
+            rows = held.tile([P, N // P, CHUNK], F32, name=f"rows{c}")
+            if c == chunks - 1:
+                nc.vector.tensor_copy(rows[:], prod[:, :, CHUNK:])
+            else:
+                nc.scalar.copy(rows[:], prod[:, :, CHUNK:])
+            places = col_list[:, c * CHUNK // LIST_ROWS : (c + 1) * CHUNK // LIST_ROWS]
+            for n, page in enumerate(pages):
+                nc.scalar.activation(page[:].indirect(places), rows[:, n, :], ACT.Copy, scale=gains[:, n : n + 1])
+
+        weigh_first(0)
+        weigh_second(0)
+        for c in range(1, chunks):
+            weigh_first(c)
+            join(c - 1)
+            weigh_second(c)
+            finish(c - 1)
+        join(chunks - 1)
+        finish(chunks - 1)
+
+        for n, page in enumerate(pages):
+            nc.sync.dma_start(out[n * P : (n + 1) * P, :], page[:])

@@ -91,6 +91,9 @@ def tile_list_softchoice_kernel(tc, xt_words, xt_scales, w_words, w_scales, w2_w
             nc.sync.dma_start(wb_rows[32 * q : 32 * q + 4, :].bitcast(I32), wb_scales[0, 4 * q : 4 * q + 4, :].bitcast(I32))
         with nc.allow_non_contiguous_dma(reason="one value a partition"):
             nc.sync.dma_start(gains[:], so.rearrange("(h p) o -> p (h o)", p=P))
+        warm = held.tile([P, 2], F32, name="warm")
+        nc.gpsimd.memset(warm[:, 0:1], 0.0)
+        nc.scalar.activation(warm[:, 1:2], warm[:, 0:1], ACT.Sigmoid)
 
         xg_words = held.tile([P, J], U16, name="xg_words", align_bytes=64)
         xg_plane = held.tile([P, J], U8, name="xg_plane", align_bytes=64)

@@ -41,8 +41,8 @@ def tile_list_softchoice_kernel(tc, xt_words, xt_scales, w_words, w_scales, w2_w
         x_plane = held.tile([P, T], U8, name="x_plane", align_bytes=64)
         store = [held.tile([P, V], U8, name=f"store{t}", align_bytes=64) for t in range(PACK)]
         w_raw = [held.tile([P, R], I32, name=f"w_raw{m}", align_bytes=64) for m in range(2)]
-        w_rows = [held.tile([P, 2 * R], U8, name=f"w_rows{m}", align_bytes=64) for m in range(2)]
-        x_rows = held.tile([4, 4 * T], U8, name="x_rows", align_bytes=64)
+        w_rows = held.tile([P, 4 * R], U8, name="w_rows", align_bytes=64)
+        x_rows = held.tile([64, 2 * T], U8, name="x_rows", align_bytes=64)
         wb_sb = held.tile([P, N], I32, name="wb_sb", align_bytes=64)
         wb_rows = held.tile([P, N], U8, name="wb_rows", align_bytes=64)
         steps = held.tile([P, PACK], F32, name="steps")
@@ -51,8 +51,12 @@ def tile_list_softchoice_kernel(tc, xt_words, xt_scales, w_words, w_scales, w2_w
         hid_words = held.tile([P, CHUNK + J], I32, name="hid_words", align_bytes=64)
         hid_plane = held.tile([P, CHUNK + J], U8, name="hid_plane", align_bytes=64)
 
-        nc.vector.memset(x_plane[:].bitcast(I32), 0)
-        for rows in (w_rows[0], w_rows[1], wb_rows):
+        nc.gpsimd.memset(x_rows[:, 0:T].bitcast(I32), 0)
+        nc.vector.memset(x_rows[:, T:].bitcast(I32), 0)
+        warm = held.tile([P, 2], F32, name="warm")
+        nc.vector.memset(warm[:, 0:1], 0.0)
+        nc.scalar.activation(warm[:, 1:2], warm[:, 0:1], ACT.Sigmoid)
+        for rows in (w_rows, wb_rows):
             nc.vector.memset(rows[:].bitcast(I32), 0)
         nc.vector.memset(hid_words[:, 0:CHUNK], 0)
         nc.vector.memset(hid_plane[:, 0:CHUNK].bitcast(I32), 0)
@@ -63,43 +67,40 @@ def tile_list_softchoice_kernel(tc, xt_words, xt_scales, w_words, w_scales, w2_w
             nc.sync.dma_start(tile[:], words[0].rearrange("p n t -> p (n t)").bitcast(I32))
 
         def load_rows(engine, rows, scales):
+            for q in range(4):
+                engine.dma_start(rows[32 * q : 32 * q + 4, :].bitcast(I32), scales[0, 4 * q : 4 * q + 4, :].bitcast(I32))
+
+        def load_row_pairs(rows, scales):
             src = scales[0].bitcast(I32).rearrange("(a b r) c -> b r a c", a=2, b=2)
             for b in range(2):
-                engine.dma_start(rows[32 * b : 32 * b + 4, :].bitcast(I32).rearrange("p (a c) -> p a c", a=2), src[b])
+                nc.sync.dma_start(rows[32 * b : 32 * b + 4], src[b])
 
-        def spread_rows(rows, width):
-            words = rows[:].bitcast(I32)
-            nc.vector.tensor_copy(words[64:128, 0 : width // 4], words[0:64, width // 4 : width // 2])
-
+        w_pairs = w_rows[:].bitcast(I32).rearrange("p (a m c) -> p a m c", a=2, m=2)
         ca_dealt = ca.rearrange("(p t) v -> t p v", t=PACK)
-        nc.sync.dma_start(x_rows[:].bitcast(I32).rearrange("r (q c) -> r q c", q=4), xt_scales[0].bitcast(I32).rearrange("(q r) c -> r q c", q=4))
         nc.sync.dma_start(tok_list[:], offs)
-        nc.sync.dma_start(x_words[:].bitcast(I32), xt_words[0].bitcast(I32))
         nc.sync.dma_start(entry_list[:], offs2)
+        nc.sync.dma_start(x_words[:].bitcast(I32), xt_words[0].bitcast(I32))
         nc.sync.dma_start(store[0][:], ca_dealt[0])
+        load_row_pairs(x_rows[:].bitcast(I32).rearrange("p (a c) -> p a c", a=2), xt_scales)
+        nc.sync.dma_start(store[1][:], ca_dealt[1])
         load_words(w_raw[0], w_words)
         load_words(w_raw[1], w2_words)
-        nc.sync.dma_start(store[1][:], ca_dealt[1])
-        nc.gpsimd.dma_start(steps[:], st.rearrange("(p t) o -> p (t o)", t=PACK))
-        load_rows(nc.sync, w_rows[0], w_scales)
-        load_rows(nc.sync, w_rows[1], w2_scales)
+        nc.sync.dma_start(steps[:], st.rearrange("(p t) o -> p (t o)", t=PACK))
+        load_row_pairs(w_pairs[:, :, 0, :], w_scales)
+        load_row_pairs(w_pairs[:, :, 1, :], w2_scales)
         nc.sync.dma_start(store[2][:], ca_dealt[2])
         nc.sync.dma_start(store[3][:], ca_dealt[3])
         load_words(wb_sb, wb_words)
         nc.sync.dma_start(col_list[:], offs3)
-        for q in range(4):
-            nc.sync.dma_start(wb_rows[32 * q : 32 * q + 4, :].bitcast(I32), wb_scales[0, 4 * q : 4 * q + 4, :].bitcast(I32))
+        load_rows(nc.sync, wb_rows, wb_scales)
         with nc.allow_non_contiguous_dma(reason="one value a partition"):
             nc.sync.dma_start(gains[:], so.rearrange("(h p) o -> p (h o)", p=P))
-        warm = held.tile([P, 2], F32, name="warm")
-        nc.gpsimd.memset(warm[:, 0:1], 0.0)
-        nc.scalar.activation(warm[:, 1:2], warm[:, 0:1], ACT.Sigmoid)
 
         xg_words = held.tile([P, J], U16, name="xg_words", align_bytes=64)
         xg_plane = held.tile([P, J], U8, name="xg_plane", align_bytes=64)
-        for q in range(4):
-            nc.vector.tensor_copy(x_plane[32 * q : 32 * q + 4, :].bitcast(I32), x_rows[:, q * T : (q + 1) * T].bitcast(I32))
         nc.vector.tensor_copy(xg_words[:], x_words[:].indirect(tok_list[:]))
+        for a in range(2):
+            nc.vector.tensor_copy(x_plane[64 * a : 64 * a + 64, :].bitcast(I32), x_rows[:, a * T : (a + 1) * T].bitcast(I32))
         nc.vector.tensor_copy(xg_plane[:], x_plane[:].indirect(tok_list[:]))
 
         w_dealt = [held.tile([P, R], U32, name=f"w_dealt{m}", align_bytes=64) for m in range(2)]
@@ -134,18 +135,19 @@ def tile_list_softchoice_kernel(tc, xt_words, xt_scales, w_words, w_scales, w2_w
             nc.scalar.copy(w_dealt[m][:].rearrange("p (t q) -> p q t", t=PACK),
                            w_raw[m][:].bitcast(U32).rearrange("p (q t) -> p q t", t=PACK))
 
-        def deal_scales(m):
-            spread_rows(w_rows[m], R)
-            nc.vector.tensor_copy(w_plane[m][:].rearrange("p (t q) -> p q t", t=PACK),
-                                  w_rows[m][:, 0:R].rearrange("p (q t) -> p q t", t=PACK))
+        def deal_scales():
+            words = w_rows[:].bitcast(I32)
+            nc.vector.tensor_copy(words[64:128, 0 : R // 2], words[0:64, R // 2 : R])
+            for m in range(2):
+                nc.vector.tensor_copy(w_plane[m][:].rearrange("p (t q) -> p t q", t=PACK),
+                                      w_rows[:, m * R : (m + 1) * R].rearrange("p (q t) -> p t q", t=PACK))
 
         deal_words(0)
-        deal_words(1)
         for t in (0, 1):
             for h in range(halves):
                 look_up(t, h)
-        deal_scales(0)
-        deal_scales(1)
+        deal_words(1)
+        deal_scales()
         for h in range(halves):
             for m in range(2):
                 first_products(m, h)
@@ -183,7 +185,7 @@ def tile_list_softchoice_kernel(tc, xt_words, xt_scales, w_words, w_scales, w2_w
                                     rhs=hid_words[:, window].bitcast(E5M2X4), rhs_scale=hid_plane[:, window],
                                     start=True, stop=True)
             rows = held.tile([P, N // P, CHUNK], F32, name=f"rows{c}")
-            if c == chunks - 1:
+            if c % 2 == 1:
                 nc.vector.tensor_copy(rows[:], prod[:, :, CHUNK:])
             else:
                 nc.scalar.copy(rows[:], prod[:, :, CHUNK:])

from contextlib import ExitStack

import concourse.mybir as mybir

K, T, J, R, V, N, E = 512, 1024, 256, 512, 1024, 256, 512
FLOPS = 2 * K * R * J * 2 + 2 * R * N * J

F32 = mybir.dt.float32
BF16 = mybir.dt.bfloat16
I32 = mybir.dt.int32
U32 = mybir.dt.uint32
U16 = mybir.dt.uint16
U8 = mybir.dt.uint8
FP8 = mybir.dt.float8_e4m3fn
E4M3X4 = mybir.dt.float8_e4m3fn_x4
E5M2X4 = mybir.dt.float8_e5m2_x4
E2M1X4 = mybir.dt.float4_e2m1fn_x4
ACT = mybir.ActivationFunctionType
ALU = mybir.AluOpType

P = 128
PACK = 4
HALF = 128
CHUNK = 64
LIST_ROWS = 16


def tile_list_softchoice_kernel(tc, xt_words, xt_scales, w_words, w_scales, w2_words, w2_scales,
                                    ca, st, wb_words, wb_scales, so, offs, offs2, offs3, out):
    nc = tc.nc
    halves = J // HALF
    chunks = J // CHUNK
    with ExitStack() as ctx:
        held = ctx.enter_context(tc.tile_pool(name="held", bufs=1))
        psum = ctx.enter_context(tc.psum_pool(name="psum", bufs=1))

        tok_list = held.tile([P, J // LIST_ROWS], U16, name="tok_list")
        entry_list = held.tile([P, J // LIST_ROWS], U16, name="entry_list")
        col_list = held.tile([P, J // LIST_ROWS], U16, name="col_list")
        x_words = held.tile([P, T], U16, name="x_words", align_bytes=64)
        x_plane = held.tile([P, T], U8, name="x_plane", align_bytes=64)
        store = [held.tile([P, V], U8, name=f"store{t}", align_bytes=64) for t in range(PACK)]
        w_raw = [held.tile([P, R], I32, name=f"w_raw{m}", align_bytes=64) for m in range(2)]
        w_rows = held.tile([P, 4 * R], U8, name="w_rows", align_bytes=64)
        x_rows = held.tile([64, 2 * T], U8, name="x_rows", align_bytes=64)
        wb_sb = held.tile([P, N], I32, name="wb_sb", align_bytes=64)
        wb_rows = held.tile([P, N], U8, name="wb_rows", align_bytes=64)
        steps = held.tile([P, PACK], F32, name="steps")
        gains = held.tile([P, N // P], F32, name="gains")
        pages = [held.tile([P, E], F32, name=f"page{n}") for n in range(N // P)]
        hid_words = held.tile([P, CHUNK + J], I32, name="hid_words", align_bytes=64)
        hid_plane = held.tile([P, CHUNK + J], U8, name="hid_plane", align_bytes=64)

        nc.gpsimd.memset(x_rows[:, 0:T].bitcast(I32), 0)
        nc.vector.memset(x_rows[:, T:].bitcast(I32), 0)
        warm = held.tile([P, 2], F32, name="warm")
        nc.vector.memset(warm[:, 0:1], 0.0)
        nc.scalar.activation(warm[:, 1:2], warm[:, 0:1], ACT.Sigmoid)
        for rows in (w_rows, wb_rows):
            nc.vector.memset(rows[:].bitcast(I32), 0)
        nc.vector.memset(hid_words[:, 0:CHUNK], 0)
        nc.vector.memset(hid_plane[:, 0:CHUNK].bitcast(I32), 0)
        for page in pages:
            nc.vector.memset(page[:], 0.0)

        def load_words(tile, words):
            nc.sync.dma_start(tile[:], words[0].rearrange("p n t -> p (n t)").bitcast(I32))

        def load_rows(engine, rows, scales):
            for q in range(4):
                engine.dma_start(rows[32 * q : 32 * q + 4, :].bitcast(I32), scales[0, 4 * q : 4 * q + 4, :].bitcast(I32))

        def load_row_pairs(rows, scales):
            src = scales[0].bitcast(I32).rearrange("(a b r) c -> b r a c", a=2, b=2)
            for b in range(2):
                nc.sync.dma_start(rows[32 * b : 32 * b + 4], src[b])

        w_pairs = w_rows[:].bitcast(I32).rearrange("p (a m c) -> p a m c", a=2, m=2)
        ca_dealt = ca.rearrange("(p t) v -> t p v", t=PACK)
        nc.sync.dma_start(tok_list[:], offs)
        nc.sync.dma_start(entry_list[:], offs2)
        nc.sync.dma_start(x_words[:].bitcast(I32), xt_words[0].bitcast(I32))
        nc.sync.dma_start(store[0][:], ca_dealt[0])
        load_row_pairs(x_rows[:].bitcast(I32).rearrange("p (a c) -> p a c", a=2), xt_scales)
        nc.sync.dma_start(store[1][:], ca_dealt[1])
        load_words(w_raw[0], w_words)
        load_words(w_raw[1], w2_words)
        nc.sync.dma_start(steps[:], st.rearrange("(p t) o -> p (t o)", t=PACK))
        load_row_pairs(w_pairs[:, :, 0, :], w_scales)
        load_row_pairs(w_pairs[:, :, 1, :], w2_scales)
        nc.sync.dma_start(store[2][:], ca_dealt[2])
        nc.sync.dma_start(store[3][:], ca_dealt[3])
        load_words(wb_sb, wb_words)
        nc.sync.dma_start(col_list[:], offs3)
        load_rows(nc.sync, wb_rows, wb_scales)
        with nc.allow_non_contiguous_dma(reason="one value a partition"):
            nc.sync.dma_start(gains[:], so.rearrange("(h p) o -> p (h o)", p=P))

        xg_words = held.tile([P, J], U16, name="xg_words", align_bytes=64)
        xg_plane = held.tile([P, J], U8, name="xg_plane", align_bytes=64)
        nc.vector.tensor_copy(xg_words[:], x_words[:].indirect(tok_list[:]))
        for a in range(2):
            nc.vector.tensor_copy(x_plane[64 * a : 64 * a + 64, :].bitcast(I32), x_rows[:, a * T : (a + 1) * T].bitcast(I32))
        nc.vector.tensor_copy(xg_plane[:], x_plane[:].indirect(tok_list[:]))

        w_dealt = [held.tile([P, R], U32, name=f"w_dealt{m}", align_bytes=64) for m in range(2)]
        w_plane = [held.tile([P, R], U8, name=f"w_plane{m}", align_bytes=64) for m in range(2)]
        sums = [[psum.tile([P, PACK, HALF], F32, name=f"sums{m}_{h}") for h in range(halves)] for m in range(2)]
        share = [held.tile([P, CHUNK, PACK], F32, name=f"share{c}") for c in range(chunks)]

        def first_products(m, h):
            cols = slice(h * HALF, (h + 1) * HALF)
            for t in range(PACK):
                nc.tensor.matmul_mx(sums[m][h][:, t, :], lhsT=w_dealt[m][:, t * P : (t + 1) * P].bitcast((E5M2X4, E4M3X4)[m]),
                                    lhsT_scale=w_plane[m][:, t * P : (t + 1) * P],
                                    rhs=xg_words[:, cols].bitcast(E2M1X4), rhs_scale=xg_plane[:, cols],
                                    start=True, stop=True)

        picked = [held.tile([P, PACK * HALF], U8, name=f"picked{h}") for h in range(halves)]
        logits = [held.tile([P, PACK, HALF], F32, name=f"logits{h}") for h in range(halves)]

        def look_up(t, h):
            entries = entry_list[:, h * HALF // LIST_ROWS : (h + 1) * HALF // LIST_ROWS]
            part = slice(t * HALF, (t + 1) * HALF)
            nc.vector.tensor_copy(picked[h][:, part], store[t][:].indirect(entries))
            nc.scalar.activation(logits[h][:, t, :], picked[h][:, part].bitcast(FP8), ACT.Copy, scale=steps[:, t : t + 1])

        def shares(h):
            for u in range(HALF // CHUNK):
                nc.scalar.activation(share[h * HALF // CHUNK + u][:].rearrange("p (c i) t -> p c t i", i=4),
                                     logits[h][:, :, u * CHUNK : (u + 1) * CHUNK].rearrange("p t (c i) -> p c t i", i=4),
                                     ACT.Sigmoid)

        def deal_words(m):
            nc.scalar.copy(w_dealt[m][:].rearrange("p (t q) -> p q t", t=PACK),
                           w_raw[m][:].bitcast(U32).rearrange("p (q t) -> p q t", t=PACK))

        def deal_scales():
            words = w_rows[:].bitcast(I32)
            nc.vector.tensor_copy(words[64:128, 0 : R // 2], words[0:64, R // 2 : R])
            for m in range(2):
                nc.vector.tensor_copy(w_plane[m][:].rearrange("p (t q) -> p t q", t=PACK),
                                      w_rows[:, m * R : (m + 1) * R].rearrange("p (q t) -> p t q", t=PACK))

        deal_words(0)
        for t in (0, 1):
            for h in range(halves):
                look_up(t, h)
        deal_words(1)
        deal_scales()
        for h in range(halves):
            for m in range(2):
                first_products(m, h)
        for h in range(halves):
            for t in (2, 3):
                look_up(t, h)
            shares(h)

        kept = [held.tile([P, CHUNK, PACK], F32, name=f"kept{c}") for c in range(4)] * chunks
        rest = [held.tile([P, CHUNK, PACK], F32, name=f"rest{c}") for c in range(4)] * chunks
        hid = [held.tile([P, CHUNK * PACK], BF16, name=f"hid{c}", align_bytes=64) for c in range(chunks)]

        def chunk_sums(m, c):
            h, u = divmod(c, HALF // CHUNK)
            return sums[m][h][:, :, u * CHUNK : (u + 1) * CHUNK].rearrange("p t j -> p j t")

        def weigh_first(c):
            nc.vector.tensor_tensor(kept[c][:], chunk_sums(0, c), share[c][:], ALU.mult)

        def weigh_second(c):
            nc.vector.scalar_tensor_tensor(rest[c][:], share[c][:], 1.0, chunk_sums(1, c), ALU.subtract, ALU.mult)

        def join(c):
            engine = nc.vector
            engine.tensor_tensor(hid[c][:], kept[c][:].rearrange("p j t -> p (j t)"), rest[c][:].rearrange("p j t -> p (j t)"), ALU.subtract)

        def finish(c):
            own = slice((c + 1) * CHUNK, (c + 2) * CHUNK)
            window = slice(c * CHUNK, (c + 2) * CHUNK)
            nc.vector.quantize_mx(hid_words[:, own].bitcast(E5M2X4), hid_plane[:, own], hid[c][:])
            prod = psum.tile([P, N // P, 2 * CHUNK], F32, name=f"prod{c}")
            for n in range(N // P):
                nc.tensor.matmul_mx(prod[:, n, :], lhsT=wb_sb[:, n * P : (n + 1) * P].bitcast(E4M3X4),
                                    lhsT_scale=wb_rows[:, n * P : (n + 1) * P],
                                    rhs=hid_words[:, window].bitcast(E5M2X4), rhs_scale=hid_plane[:, window],
                                    start=True, stop=True)
            rows = held.tile([P, N // P, CHUNK], F32, name=f"rows{c}")
            if c % 2 == 1:
                nc.vector.tensor_copy(rows[:], prod[:, :, CHUNK:])
            else:
                nc.scalar.copy(rows[:], prod[:, :, CHUNK:])
            places = col_list[:, c * CHUNK // LIST_ROWS : (c + 1) * CHUNK // LIST_ROWS]
            for n, page in enumerate(pages):
                nc.scalar.activation(page[:].indirect(places), rows[:, n, :], ACT.Copy, scale=gains[:, n : n + 1])

        weigh_first(0)
        weigh_second(0)
        for c in range(1, chunks):
            weigh_first(c)
            join(c - 1)
            weigh_second(c)
            finish(c - 1)
        join(chunks - 1)
        finish(chunks - 1)

        for n, page in enumerate(pages):
            nc.sync.dma_start(out[n * P : (n + 1) * P, :], page[:])
